import numpy as np
import ml_dtypes


def mxq(x, axis, fmt="e4m3"):
    dtype, down = {"e4m3": (ml_dtypes.float8_e4m3fn, 7), "e5m2": (ml_dtypes.float8_e5m2, 14)}[fmt]
    v = np.moveaxis(np.asarray(x, np.float32).astype(ml_dtypes.bfloat16).astype(np.float64), axis, -1)
    blocks = v.reshape(v.shape[:-1] + (-1, 32))
    amax = np.abs(blocks).max(-1, keepdims=True)
    byte = np.maximum(np.where(amax > 0, np.frexp(amax)[1] - 1 + 127, 0) - down, 1)
    scale = np.exp2(byte - 127.0)
    codes = (blocks / scale).astype(np.float32).astype(dtype).astype(np.float64)
    return np.moveaxis((codes * scale).reshape(v.shape), -1, axis)


WIDE = False


def mx_kscale(k):
    if not WIDE:
        return np.ones(k)
    levels = np.array([10, -10, 5, -5, 0])
    if k % 512:
        return np.exp2(np.random.permutation(np.resize(levels, k // 32))).repeat(32)
    a = np.empty((k // 512, 16))
    for p in range(k // 512):
        a[p, :8] = np.random.permutation(np.resize(levels, 8))
        for g in range(8):
            far = levels[np.abs(levels - a[p, g]) >= 10]
            a[p, g + 8] = far[np.random.randint(len(far))]
    return np.exp2(a.ravel()).repeat(32)


BF16 = ml_dtypes.bfloat16


def bf(x):
    return np.asarray(x, np.float32).astype(BF16)


def f64(x):
    return np.asarray(x).astype(np.float64)


E2M1 = np.array([0.0, 0.5, 1.0, 1.5, 2.0, 3.0, 4.0, 6.0, -0.0, -0.5, -1.0, -1.5, -2.0, -3.0, -4.0, -6.0])


def pack_weight(w, fmt):
    k, n = w.shape
    w = f64(bf(w)).reshape(k // 32, 32, n)
    amax = np.abs(w).max(1)
    if fmt == "e4m3":
        byte = np.frexp(amax)[1] - 1 + 127 - 7
    else:
        mant, ex = np.frexp(amax / 6.0)
        byte = np.where(mant > 0.5, ex, ex - 1) + 127
    byte = np.clip(np.where(amax > 0, byte, 1), 1, 254)
    scaled = (w * np.exp2(127.0 - byte)[:, None, :]).reshape(k, n).astype(np.float32)
    by_word = np.ascontiguousarray(scaled.reshape(k // 512, 128, 4, n).transpose(0, 1, 3, 2))
    if fmt == "e4m3":
        words = by_word.astype(ml_dtypes.float8_e4m3fn).view(np.uint8)
    else:
        c = by_word.astype(ml_dtypes.float4_e2m1fn).view(np.uint8) & 0xF
        words = c[..., 0::2] | (c[..., 1::2] << 4)
    return np.ascontiguousarray(words), np.ascontiguousarray(byte.astype(np.uint8).reshape(k // 512, 16, n))


def unpack_weight(words, scales, fmt):
    g, p, n, _ = words.shape
    if fmt == "e4m3":
        vals = np.ascontiguousarray(words).view(ml_dtypes.float8_e4m3fn).astype(np.float64)
    else:
        nib = np.empty((g, p, n, 4), np.uint8)
        nib[..., 0::2] = words & 0xF
        nib[..., 1::2] = words >> 4
        vals = E2M1[nib]
    vals = vals * np.repeat(np.exp2(scales.astype(np.float64) - 127.0), 8, axis=1)[..., None]
    return vals.transpose(0, 1, 3, 2).reshape(g * 512, n)
def pack4(w):
    words, scales = pack_weight(w, "e2m1")
    return words.reshape(words.shape[0], 128, -1), scales


def unpack4(words, scales):
    return unpack_weight(words.reshape(words.shape[0], 128, -1, 2), scales, "e2m1")


M, N, R = 1024, 1024, 2048

GAIN = 0.45
SPREAD = 0.1


def setup_inputs():
    s = mx_kscale(N)
    w1_words, w1_scales = pack4(np.random.standard_normal((N, N)) / np.sqrt(N) / s[:, None])
    w2_words, w2_scales = pack4(np.random.standard_normal((N, N)) / np.sqrt(N) / s[:, None])
    w3_words, w3_scales = pack4(np.random.standard_normal((N, R)) / np.sqrt(N) / s[:, None])
    return {"rates": bf(np.abs(np.random.standard_normal((M, N))) * s),
            "gain1": bf((GAIN + SPREAD * np.random.standard_normal(N)) * s),
            "gain2": bf((GAIN + SPREAD * np.random.standard_normal(N)) * s),
            "w1_words": w1_words, "w1_scales": w1_scales,
            "w2_words": w2_words, "w2_scales": w2_scales,
            "w3_words": w3_words, "w3_scales": w3_scales}


def reference(rates, gain1, gain2, w1_words, w1_scales, w2_words, w2_scales, w3_words, w3_scales):
    r0 = f64(rates)
    u1 = mxq(r0, 1, "e4m3") @ unpack4(w1_words, w1_scales)
    r1 = r0 + f64(gain1) * np.maximum(u1, 0.0)
    u2 = mxq(r1, 1, "e4m3") @ unpack4(w2_words, w2_scales)
    r2 = r1 + f64(gain2) * np.maximum(u2, 0.0)
    return mxq(r2, 1, "e4m3") @ unpack4(w3_words, w3_scales)

@@ -1,0 +1,313 @@
+from contextlib import ExitStack
+
+import concourse.mybir as mybir
+from concourse.masks import make_identity
+
+TRIALS, NEURONS, TARGETS = 1024, 1024, 2048
+SINGLE = ()
+FLOPS = 2 * TRIALS * NEURONS * (2 * NEURONS + TARGETS)
+
+F32 = mybir.dt.float32
+BF16 = mybir.dt.bfloat16
+U32 = mybir.dt.uint32
+I32 = mybir.dt.int32
+U8 = mybir.dt.uint8
+E4M3 = mybir.dt.float8_e4m3fn_x4
+E2M1 = mybir.dt.float4_e2m1fn_x4
+ACT = mybir.ActivationFunctionType
+ALU = mybir.AluOpType
+
+P = 128
+G = 2
+T = 4
+CHUNKS = (512, 512,)
+ORDER = """
+Dp10 Ds10 PT1 Ds11 PT2 AC1 Dp11 PT0 PT3 AC0 DC2 PT5 AC3 PT4
+Dq000 PT6 AC4 Dq001 PT7 AC6 Ds20 PM1001 AC7 Dp20 PM1003 AR1001 PM1012 AC5
+Dp21 PM1011 AR1003 PM1010 AR1012 Dq010 PM1002 AR1011 Dq011 PM1000 AR1002 DX1011 PM1111 AR1010
+DX1001 PM1013 AR1000 DX1003 PM1101 AR1013 DX1012 PM1100 AR1111 DX1000 PM1110 AR1101 DX1002 PM1112
+AR1100 Ds21 PM1103 AG1001 DX1010 PM1102 DX1013 PM1113 DG1000 AG1011 DX1100 DG1010 AR1113 Dq100
+AR1103 Dq101 AR1102 PM2013 DX1101 PM2010 AR2013 DX1113 PM2011 AR1112 DX1102 DX1103 AR1110 DX1112
+AR2011 PM2003 DX1110 AG1100 PM2002 DX1111 PM2001 DG1101 PM2012 AR2010 DG1111 PM2000 AG1110 Dq110
+DX2010 AR2000 Dq111 AR2001 PM2110 DX2000 AR2012 PM2101 DX2013 AR2002 PM2112 DX2001 AR2003 DX2012
+AR2110 PM2111 DX2011 AR2112 PM2113 DX2003 AG2011 PM2103 DX2002 DG2010 PM2102 PM2100 DG2001 AR2103
+DG2000 AR2101 Dq201 AR2100 Dq200 AR2113 AR2111 PY00 DX2113 AR2102 PY01 DX2100 AO00 PY02
+DX2112 AO01 PY03 DX2103 AO02 PY04 DX2111 AO03 PY05 DX2110 AO04 PY06 DX2101 PY07
+AO05 DG2111 PY08 AO06 DX2102 PY09 AO07 DG2110 PY10 AO08 DG2101 PY11 AO10 DG2100
+PY12 AO11 Dq210 PY13 AO09 Dq211 AO12 PY16 AO13 PY17 AO16 PY18 AO17 PY19
+AO18 PY20 DO19 PY21 AO20 PY22 AO21 PY23 AO22 PY24 AO23 PY25 DO24 PY26
+DO25 PY14 DO26 PY27 DO14 PY28 AO27 PY29 AO28 PY30 AO29 PY15 DO30 PY31
+DO15 AO31
+"""
+
+
+def tile_theta_phase_rates_t2_kernel(
+    tc, rates, gain1, gain2, w1_words, w1_scales, w2_words, w2_scales, w3_words, w3_scales, out
+):
+    nc = tc.nc
+    with ExitStack() as ctx:
+        keep = ctx.enter_context(tc.tile_pool(name="keep", bufs=1))
+        work = ctx.enter_context(tc.tile_pool(name="work", bufs=2))
+        psum = ctx.enter_context(tc.psum_pool(name="psum", bufs=8))
+        ctx.enter_context(tc.manual_schedule())
+
+        def const(name, shape, dtype):
+            return keep.tile(shape, dtype, name=name, align_bytes=256)
+
+        raw_w = {}
+        raw_s = {}
+        for i in (1, 2, 3):
+            n = TARGETS if i == 3 else NEURONS
+            raw_w[i] = const(f"raw_w{i}", [P, G, 2 * n], U8)
+            raw_s[i] = const(f"raw_s{i}", [P, G, n], U8)
+        words_in = {1: w1_words, 2: w2_words, 3: w3_words}
+        scales_in = {1: w1_scales, 2: w2_scales, 3: w3_scales}
+        ident = const("ident", [P, P], F32)
+        make_identity(nc, ident[:])
+        for i in (1, 2, 3):
+            nc.vector.memset(raw_s[i][:].rearrange("p g n -> p (g n)").bitcast(I32), 0)
+
+        gains = {}
+        for i, g_in in ((1, gain1), (2, gain2)):
+            gains[i] = const(f"gain{i}", [P, G, T], BF16)
+
+        def load_scales(i):
+            src = scales_in[i].bitcast(I32)
+            for q in range(4):
+                nc.sync.dma_start(
+                    out=raw_s[i][32 * q : 32 * q + 4, :, :].bitcast(I32),
+                    in_=src[:, 4 * q : 4 * q + 4, :].rearrange("g q n -> q g n"),
+                )
+
+        def load_words(i):
+            nc.sync.dma_start(
+                out=raw_w[i][:].bitcast(I32), in_=words_in[i].bitcast(I32).rearrange("g p n -> p g n")
+            )
+
+        n_blocks = TRIALS // P
+        x = {}
+
+        def load_block(b):
+            x[b] = const(f"x{b}", [P, NEURONS], BF16)
+            nc.sync.dma_start(out=x[b][:], in_=rates[b * P : (b + 1) * P, :])
+
+        def load_gain(i, g_in):
+            nc.sync.dma_start(out=gains[i][:], in_=g_in.rearrange("(g p t) -> p g t", g=G, t=T))
+
+        load_gain_q = nc.scalar
+        for i, g_in in ((1, gain1), (2, gain2)):
+            load_gain_q.dma_start(out=gains[i][:], in_=g_in.rearrange("(g p t) -> p g t", g=G, t=T))
+        load_scales(1)
+        load_words(1)
+        for b in range(n_blocks):
+            load_block(b)
+        load_scales(2)
+        load_words(2)
+        load_scales(3)
+        load_words(3)
+
+        size = {}
+        sign = {}
+
+        def prepare_gain(i):
+            flat = gains[i][:].rearrange("p g t -> p (g t)")
+            size[i] = const(f"size{i}", [P, G * T], F32)
+            sign[i] = const(f"sign{i}", [P, G * T], F32)
+            nc.scalar.activation(out=size[i][:], in_=flat, func=ACT.Abs)
+            nc.vector.tensor_scalar(
+                out=sign[i][:], in0=flat, scalar1=0.0, scalar2=2.0, op0=ALU.is_ge, op1=ALU.mult
+            )
+            nc.vector.tensor_scalar_add(sign[i][:], sign[i][:], -1.0)
+
+        per_w = {}
+        per_s = {}
+        for i in (1, 2):
+            per_w[i] = const(f"per_w{i}", [P, G, G, T, P, 2], U8)
+            per_s[i] = const(f"per_s{i}", [P, G, G, T, P], U8)
+
+        def permute_words(i, h):
+            for g in range(G):
+                nc.vector.tensor_copy(
+                    out=per_w[i][:, g, h, :, :, :],
+                    in_=raw_w[i][:, g, 1024 * h : 1024 * h + 1024].rearrange("p (j t b) -> p t j b", t=T, b=2),
+                )
+
+        def permute_scales(i, h):
+            nc.vector.tensor_copy(
+                out=per_s[i][:, :, h, :, :],
+                in_=raw_s[i][:, :, 512 * h : 512 * h + 512].rearrange("p g (j t) -> p g t j", t=T),
+            )
+
+        starts = [sum(CHUNKS[:c]) for c in range(len(CHUNKS))]
+        rt = {}
+        codes = {}
+        planes = {}
+        r1 = {}
+        for c, width in enumerate(CHUNKS):
+            rt[c] = const(f"rt{c}", [P, G, width, T], BF16)
+            r1[c] = const(f"r1_{c}", [P, G, T, width], F32)
+            for s in (0, 1, 2):
+                codes[s, c] = const(f"codes{s}_{c}", [P, G, width], U32)
+                planes[s, c] = const(f"planes{s}_{c}", [P, G, width], U8)
+
+        def bank():
+            return psum.tile([P, 512], F32, name="bank")
+
+        def copy_out(use_v, dst, src):
+            if use_v:
+                nc.vector.tensor_copy(out=dst, in_=src)
+            else:
+                nc.scalar.copy(out=dst, in_=src)
+
+        def words_out(c):
+            return rt[c][:].rearrange("p g m t -> p (g m t)").bitcast(F32).rearrange("p (g m u) -> p g m u", g=G, u=2)
+
+        banks = {}
+
+        def transpose(blk):
+            words = x[blk][:].bitcast(F32)
+            acc = banks[blk] = bank()
+            for g in range(G):
+                for u in range(2):
+                    k = 2 * g + u
+                    nc.tensor.transpose(
+                        acc[:, k * P : (k + 1) * P], words[:, 256 * g + u : 256 * (g + 1) : 2], ident[:]
+                    )
+
+        def chunk_of(blk):
+            c = max(c for c in range(len(CHUNKS)) if starts[c] <= blk * P)
+            return c, blk - starts[c] // P
+
+        def copy_turned(use_v, blk):
+            c, b = chunk_of(blk)
+            copy_out(
+                use_v,
+                words_out(c)[:, :, b * P : (b + 1) * P, :],
+                banks.pop(blk)[:].rearrange("p (g u m) -> p g m u", g=G, u=2),
+            )
+
+        def quantise(s, c, g):
+            src = rt[c][:, g, :, :] if s == 0 else grouped.pop((s, c, g))[:]
+            nc.vector.quantize_mx(
+                out=codes[s, c][:, g, :].bitcast(E4M3), scales=planes[s, c][:, g, :], in_=src.rearrange("p m t -> p (m t)")
+            )
+
+        v = {}
+        r2 = {}
+        grouped = {}
+
+        def multiply(s, c, h, t):
+            width = CHUNKS[c]
+            step = 512 if width == 512 else 128
+            acc = banks[s, c, h, t] = bank()
+            for n0 in range(0, width, step):
+                for g in range(G):
+                    nc.tensor.matmul_mx(
+                        out=acc[:, n0 : n0 + step],
+                        lhsT=per_w[s][:, g, h, t, :, :].rearrange("p j b -> p (j b)").bitcast(E2M1),
+                        lhsT_scale=per_s[s][:, g, h, t, :],
+                        rhs=codes[s - 1, c][:, g, n0 : n0 + step].bitcast(E4M3),
+                        rhs_scale=planes[s - 1, c][:, g, n0 : n0 + step],
+                        start=(g == 0),
+                        stop=(g == G - 1),
+                    )
+
+        def relu(s, c, h, t):
+            width = CHUNKS[c]
+            if (s, c, h) not in v:
+                v[s, c, h] = work.tile([P, T, width], F32, name="v", bufs=4)
+            j = h * T + t
+            nc.scalar.activation(
+                out=v[s, c, h][:, t, :],
+                in_=banks.pop((s, c, h, t))[:, :width],
+                func=ACT.Relu,
+                scale=size[s][:, j : j + 1],
+            )
+
+        def add(s, c, h, t):
+            if s == 2 and (c, h) not in r2:
+                r2[c, h] = work.tile([P, T, CHUNKS[c]], BF16, name="r2", bufs=3)
+            j = h * T + t
+            nc.vector.scalar_tensor_tensor(
+                out=r1[c][:, h, t, :] if s == 1 else r2[c, h][:, t, :],
+                in0=v[s, c, h][:, t, :],
+                scalar=sign[s][:, j : j + 1],
+                in1=rt[c][:, h, :, t] if s == 1 else r1[c][:, h, t, :],
+                op0=ALU.mult,
+                op1=ALU.add,
+            )
+
+        def cast(use_v, s, c, h, part):
+            width = CHUNKS[c]
+            parts = 2 if width == 512 else 1
+            if (s, c, h) not in grouped:
+                grouped[s, c, h] = work.tile([P, width, T], BF16, name="grouped", align_bytes=64, bufs=4)
+            run = 4 if s == 1 else 8
+            src = r1[c][:, h, :, :] if s == 1 else r2[c, h][:]
+            m = slice(width // parts * part, width // parts * (part + 1))
+            copy_out(
+                use_v,
+                grouped[s, c, h][:, m, :].rearrange("p (c i) t -> p c t i", i=run),
+                src[:, :, m].rearrange("p t (c i) -> p c t i", i=run),
+            )
+
+        ys = {}
+
+        def y_mul(i):
+            b, n = divmod(i, 4)
+            c, m0 = chunk_of(b)
+            m = slice(m0 * P, (m0 + 1) * P)
+            acc = banks["y", i] = bank()
+            for g in range(G):
+                nc.tensor.matmul_mx(
+                    out=acc[:],
+                    lhsT=codes[2, c][:, g, m].bitcast(E4M3),
+                    lhsT_scale=planes[2, c][:, g, m],
+                    rhs=raw_w[3][:, g, 1024 * n : 1024 * n + 1024].bitcast(E2M1),
+                    rhs_scale=raw_s[3][:, g, 512 * n : 512 * n + 512],
+                    start=(g == 0),
+                    stop=(g == G - 1),
+                )
+
+        def y_out(use_v, i):
+            b, n = divmod(i, 4)
+            pair = i // 2
+            if pair not in ys:
+                ys[pair] = [work.tile([P, 1024], F32, name="y", bufs=8), 0]
+            ys[pair][1] += 1
+            half = slice(512 * (n % 2), 512 * (n % 2) + 512)
+            copy_out(use_v, ys[pair][0][:, half], banks.pop(("y", i))[:])
+            if i in SINGLE:
+                nc.sync.dma_start(out=out[b * P : (b + 1) * P, 512 * n : 512 * n + 512], in_=ys[pair][0][:, half])
+            elif ys[pair][1] == 2:
+                both = slice(1024 * (n // 2), 1024 * (n // 2) + 1024)
+                nc.sync.dma_start(out=out[b * P : (b + 1) * P, both], in_=ys[pair][0][:])
+
+        prepare_gain(1)
+        prepare_gain(2)
+        for token in ORDER.split():
+            use_v = token[0] == "D"
+            kind = token[1]
+            a = [int(ch) for ch in token[2:]]
+            if kind == "p":
+                permute_words(*a)
+            elif kind == "s":
+                permute_scales(*a)
+            elif kind == "T":
+                transpose(*a)
+            elif kind == "C":
+                copy_turned(use_v, *a)
+            elif kind == "q":
+                quantise(*a)
+            elif kind == "M":
+                multiply(*a)
+            elif kind == "R":
+                relu(*a)
+            elif kind == "X":
+                add(*a)
+            elif kind == "G":
+                cast(use_v, *a)
+            elif kind == "Y":
+                y_mul(a[0] * 10 + a[1])
+            elif kind == "O":
+                y_out(use_v, a[0] * 10 + a[1])

@@ -20,24 +20,25 @@ ALU = mybir.AluOpType
 P = 128
 G = 2
 T = 4
-CHUNKS = (512, 512,)
+CHUNKS = (512, 512)
 ORDER = """
-Dp10 Ds10 PT1 Ds11 PT2 AC1 Dp11 PT0 PT3 AC0 DC2 PT5 AC3 PT4
-Dq000 PT6 AC4 Dq001 PT7 AC6 Ds20 PM1001 AC7 Dp20 PM1003 AR1001 PM1012 AC5
-Dp21 PM1011 AR1003 PM1010 AR1012 Dq010 PM1002 AR1011 Dq011 PM1000 AR1002 DX1011 PM1111 AR1010
-DX1001 PM1013 AR1000 DX1003 PM1101 AR1013 DX1012 PM1100 AR1111 DX1000 PM1110 AR1101 DX1002 PM1112
-AR1100 Ds21 PM1103 AG1001 DX1010 PM1102 DX1013 PM1113 DG1000 AG1011 DX1100 DG1010 AR1113 Dq100
-AR1103 Dq101 AR1102 PM2013 DX1101 PM2010 AR2013 DX1113 PM2011 AR1112 DX1102 DX1103 AR1110 DX1112
-AR2011 PM2003 DX1110 AG1100 PM2002 DX1111 PM2001 DG1101 PM2012 AR2010 DG1111 PM2000 AG1110 Dq110
-DX2010 AR2000 Dq111 AR2001 PM2110 DX2000 AR2012 PM2101 DX2013 AR2002 PM2112 DX2001 AR2003 DX2012
-AR2110 PM2111 DX2011 AR2112 PM2113 DX2003 AG2011 PM2103 DX2002 DG2010 PM2102 PM2100 DG2001 AR2103
-DG2000 AR2101 Dq201 AR2100 Dq200 AR2113 AR2111 PY00 DX2113 AR2102 PY01 DX2100 AO00 PY02
-DX2112 AO01 PY03 DX2103 AO02 PY04 DX2111 AO03 PY05 DX2110 AO04 PY06 DX2101 PY07
-AO05 DG2111 PY08 AO06 DX2102 PY09 AO07 DG2110 PY10 AO08 DG2101 PY11 AO10 DG2100
-PY12 AO11 Dq210 PY13 AO09 Dq211 AO12 PY16 AO13 PY17 AO16 PY18 AO17 PY19
-AO18 PY20 DO19 PY21 AO20 PY22 AO21 PY23 AO22 PY24 AO23 PY25 DO24 PY26
-DO25 PY14 DO26 PY27 DO14 PY28 AO27 PY29 AO28 PY30 AO29 PY15 DO30 PY31
-DO15 AO31
+Dp10 PT0 Ds10 PT1 AC0 PT2 DC1 PT3 DC2 PT4 AC3 Dp11 PT5 AC4
+PT6 AC5 Dq000 PT7 AC6 Dq001 PM1000 AC7 Ds11 PM1001 Dq010 AR1000 PM1010 Dq011
+AR1001 PM1002 Ds20 AR1010 PM1011 DX1000 AR1002 PM1003 DX1001 AR1011 PM1012 DX1010 AR1003 PM1013
+DX1002 AR1012 PM1110 DX1003 AR1013 PM1100 DX1011 AG1001 PM1101 DG1000 PM1111 DX1012 AR1110 PM1102
+DX1013 AR1111 PM1103 Dq100 AG1011 PM1112 DG1010 PM1113 Dp20 AR1100 AR1101 Dq101 PM2000 AR1102
+Dp21 AR1112 Ds21 AR2000 DX1100 AR1113 PM2010 DX1110 AR1103 PM2001 DX1101 AR2010a PM2002 AR2001
+DX1102 PM2011 AR2002 DX1103 PM2003 DX1111 AG1100 PM2012 DX1112 PM2013 DX1113 AR2011a DG1101 AG1111
+DX2010a Dq110 AR2003 DG1110 AR2012a DX2011a AR2013a Dq111 AR2010b PM2100 DX2012a AR2011b DX2000 AR2012b
+PM2110 AR2100 DX2013a PM2111 DX2001 AR2110a PM2101 AR2013b DX2002 AR2111a PM2112 AR2110b DX2003 AR2101
+PM2113 DG2010 AR2111b PM2102 AR2112b DG2000 AR2113b PM2103 Dq2010 AR2102 Dq2000 DX2010b AR2112a PY00
+DX2011b AR2113a DX2012b PY01 AR2103 DX2110a DO00 PY02 AO01 DX2013b PY03 AO02 DG2001 PY04
+AO03 DG2011 PY05 AO04 Dq2001 PY06 Dq2011 AO05 DX2100 PY07 AO06 DX2101 PY08 AO07
+DX2111a PY09 AO08 DX2102 PY10 AO09 DX2103 PY11 AO10 DX2112a DX2113a PY12 AO11 DG2100
+PY13 AO12 DG2110 PY14 AO13 Dq2100 PY15 Dq2110 AO14 DX2110b PY16 DX2111b AO15 DG2101
+PY17 AO16 DX2112b PY18 Dq2101 AO17 DX2113b PY19 AO18 DG2111 PY20 AO19 PY21 Dq2111
+AO20 PY22 AO21 PY23 AO22 PY24 AO23 PY25 DO24 PY26 DO25 PY27 AO26 PY28
+DO27 PY29 DO28 PY30 DO29 PY31 AO30 AO31
 """
 
 
@@ -71,40 +72,50 @@ def tile_theta_phase_rates_t2_kernel(
         for i, g_in in ((1, gain1), (2, gain2)):
             gains[i] = const(f"gain{i}", [P, G, T], BF16)
 
-        def load_scales(i):
+        def load_scales(i, queue):
             src = scales_in[i].bitcast(I32)
             for q in range(4):
-                nc.sync.dma_start(
+                queue.dma_start(
                     out=raw_s[i][32 * q : 32 * q + 4, :, :].bitcast(I32),
                     in_=src[:, 4 * q : 4 * q + 4, :].rearrange("g q n -> q g n"),
                 )
 
-        def load_words(i):
+        def load_words(i, part, parts):
+            size_w = words_in[i].shape[2] // 4 // parts
+            cols = slice(size_w * part, size_w * (part + 1))
             nc.sync.dma_start(
-                out=raw_w[i][:].bitcast(I32), in_=words_in[i].bitcast(I32).rearrange("g p n -> p g n")
+                out=raw_w[i][:].rearrange("p g n -> p (g n)").bitcast(I32).rearrange("p (g n) -> p g n", g=G)[:, :, cols],
+                in_=words_in[i].bitcast(I32)[:, :, cols].rearrange("g p n -> p g n"),
             )
 
         n_blocks = TRIALS // P
         x = {}
 
-        def load_block(b):
-            x[b] = const(f"x{b}", [P, NEURONS], BF16)
-            nc.sync.dma_start(out=x[b][:], in_=rates[b * P : (b + 1) * P, :])
+        def load_blocks(b, count):
+            tile = const(f"x{b}", [P, count, NEURONS], BF16)
+            for i in range(count):
+                x[b + i] = tile[:, i, :]
+            nc.sync.dma_start(
+                out=tile[:], in_=rates[b * P : (b + count) * P, :].rearrange("(i p) n -> p i n", p=P)
+            )
 
         def load_gain(i, g_in):
             nc.sync.dma_start(out=gains[i][:], in_=g_in.rearrange("(g p t) -> p g t", g=G, t=T))
 
-        load_gain_q = nc.scalar
         for i, g_in in ((1, gain1), (2, gain2)):
-            load_gain_q.dma_start(out=gains[i][:], in_=g_in.rearrange("(g p t) -> p g t", g=G, t=T))
-        load_scales(1)
-        load_words(1)
-        for b in range(n_blocks):
-            load_block(b)
-        load_scales(2)
-        load_words(2)
-        load_scales(3)
-        load_words(3)
+            nc.gpsimd.dma_start(out=gains[i][:], in_=g_in.rearrange("(g p t) -> p g t", g=G, t=T))
+        load_words(1, 0, 2)
+        load_blocks(0, 1)
+        load_scales(1, nc.sync)
+        load_blocks(1, 1)
+        load_blocks(2, 2)
+        load_words(1, 1, 2)
+        load_blocks(4, 2)
+        load_blocks(6, 2)
+        load_scales(2, nc.sync)
+        load_words(2, 0, 1)
+        load_scales(3, nc.sync)
+        load_words(3, 0, 1)
 
         size = {}
         sign = {}
@@ -165,7 +176,7 @@ def tile_theta_phase_rates_t2_kernel(
         banks = {}
 
         def transpose(blk):
-            words = x[blk][:].bitcast(F32)
+            words = x[blk].bitcast(F32)
             acc = banks[blk] = bank()
             for g in range(G):
                 for u in range(2):
@@ -186,10 +197,11 @@ def tile_theta_phase_rates_t2_kernel(
                 banks.pop(blk)[:].rearrange("p (g u m) -> p g m u", g=G, u=2),
             )
 
-        def quantise(s, c, g):
-            src = rt[c][:, g, :, :] if s == 0 else grouped.pop((s, c, g))[:]
+        def quantise(s, c, g, half=None):
+            m = half_of(CHUNKS[c], half)
+            src = rt[c][:, g, m, :] if s == 0 else grouped[s, c, g][:, m, :]
             nc.vector.quantize_mx(
-                out=codes[s, c][:, g, :].bitcast(E4M3), scales=planes[s, c][:, g, :], in_=src.rearrange("p m t -> p (m t)")
+                out=codes[s, c][:, g, m].bitcast(E4M3), scales=planes[s, c][:, g, m], in_=src.rearrange("p m t -> p (m t)")
             )
 
         v = {}
@@ -212,27 +224,31 @@ def tile_theta_phase_rates_t2_kernel(
                         stop=(g == G - 1),
                     )
 
-        def relu(s, c, h, t):
+        def half_of(width, half):
+            return slice(0, width) if half is None else slice(width // 2 * half, width // 2 * (half + 1))
+
+        def relu(s, c, h, t, half):
             width = CHUNKS[c]
-            if (s, c, h) not in v:
-                v[s, c, h] = work.tile([P, T, width], F32, name="v", bufs=4)
+            m = half_of(width, half)
+            v[s, c, h, t, half] = work.tile([P, width], F32, name="v", bufs=15)
             j = h * T + t
             nc.scalar.activation(
-                out=v[s, c, h][:, t, :],
-                in_=banks.pop((s, c, h, t))[:, :width],
+                out=v[s, c, h, t, half][:, m],
+                in_=banks[s, c, h, t][:, m],
                 func=ACT.Relu,
                 scale=size[s][:, j : j + 1],
             )
 
-        def add(s, c, h, t):
+        def add(s, c, h, t, half):
+            m = half_of(CHUNKS[c], half)
             if s == 2 and (c, h) not in r2:
-                r2[c, h] = work.tile([P, T, CHUNKS[c]], BF16, name="r2", bufs=3)
+                r2[c, h] = work.tile([P, T, CHUNKS[c]], BF16, name="r2", bufs=4)
             j = h * T + t
             nc.vector.scalar_tensor_tensor(
-                out=r1[c][:, h, t, :] if s == 1 else r2[c, h][:, t, :],
-                in0=v[s, c, h][:, t, :],
+                out=r1[c][:, h, t, m] if s == 1 else r2[c, h][:, t, m],
+                in0=v[s, c, h, t, half][:, m],
                 scalar=sign[s][:, j : j + 1],
-                in1=rt[c][:, h, :, t] if s == 1 else r1[c][:, h, t, :],
+                in1=rt[c][:, h, m, t] if s == 1 else r1[c][:, h, t, m],
                 op0=ALU.mult,
                 op1=ALU.add,
             )
@@ -273,7 +289,7 @@ def tile_theta_phase_rates_t2_kernel(
             b, n = divmod(i, 4)
             pair = i // 2
             if pair not in ys:
-                ys[pair] = [work.tile([P, 1024], F32, name="y", bufs=8), 0]
+                ys[pair] = [work.tile([P, 1024], F32, name="y", bufs=7), 0]
             ys[pair][1] += 1
             half = slice(512 * (n % 2), 512 * (n % 2) + 512)
             copy_out(use_v, ys[pair][0][:, half], banks.pop(("y", i))[:])
@@ -283,12 +299,16 @@ def tile_theta_phase_rates_t2_kernel(
                 both = slice(1024 * (n // 2), 1024 * (n // 2) + 1024)
                 nc.sync.dma_start(out=out[b * P : (b + 1) * P, both], in_=ys[pair][0][:])
 
-        prepare_gain(1)
-        prepare_gain(2)
+        ready = False
         for token in ORDER.split():
             use_v = token[0] == "D"
             kind = token[1]
-            a = [int(ch) for ch in token[2:]]
+            half = {"a": 0, "b": 1}.get(token[-1])
+            a = [int(ch) for ch in token[2:] if ch not in "ab"]
+            if kind == "R" and not ready:
+                prepare_gain(1)
+                prepare_gain(2)
+                ready = True
             if kind == "p":
                 permute_words(*a)
             elif kind == "s":
@@ -302,9 +322,9 @@ def tile_theta_phase_rates_t2_kernel(
             elif kind == "M":
                 multiply(*a)
             elif kind == "R":
-                relu(*a)
+                relu(*a, half)
             elif kind == "X":
-                add(*a)
+                add(*a, half)
             elif kind == "G":
                 cast(use_v, *a)
             elif kind == "Y":

@@ -4,7 +4,7 @@ import concourse.mybir as mybir
 from concourse.masks import make_identity
 
 TRIALS, NEURONS, TARGETS = 1024, 1024, 2048
-SINGLE = ()
+SINGLE = (30, 31)
 FLOPS = 2 * TRIALS * NEURONS * (2 * NEURONS + TARGETS)
 
 F32 = mybir.dt.float32
@@ -22,23 +22,23 @@ G = 2
 T = 4
 CHUNKS = (512, 512)
 ORDER = """
-Dp10 PT0 Ds10 PT1 AC0 PT2 DC1 PT3 DC2 PT4 AC3 Dp11 PT5 AC4
-PT6 AC5 Dq000 PT7 AC6 Dq001 PM1000 AC7 Ds11 PM1001 Dq010 AR1000 PM1010 Dq011
-AR1001 PM1002 Ds20 AR1010 PM1011 DX1000 AR1002 PM1003 DX1001 AR1011 PM1012 DX1010 AR1003 PM1013
-DX1002 AR1012 PM1110 DX1003 AR1013 PM1100 DX1011 AG1001 PM1101 DG1000 PM1111 DX1012 AR1110 PM1102
-DX1013 AR1111 PM1103 Dq100 AG1011 PM1112 DG1010 PM1113 Dp20 AR1100 AR1101 Dq101 PM2000 AR1102
-Dp21 AR1112 Ds21 AR2000 DX1100 AR1113 PM2010 DX1110 AR1103 PM2001 DX1101 AR2010a PM2002 AR2001
-DX1102 PM2011 AR2002 DX1103 PM2003 DX1111 AG1100 PM2012 DX1112 PM2013 DX1113 AR2011a DG1101 AG1111
-DX2010a Dq110 AR2003 DG1110 AR2012a DX2011a AR2013a Dq111 AR2010b PM2100 DX2012a AR2011b DX2000 AR2012b
-PM2110 AR2100 DX2013a PM2111 DX2001 AR2110a PM2101 AR2013b DX2002 AR2111a PM2112 AR2110b DX2003 AR2101
-PM2113 DG2010 AR2111b PM2102 AR2112b DG2000 AR2113b PM2103 Dq2010 AR2102 Dq2000 DX2010b AR2112a PY00
-DX2011b AR2113a DX2012b PY01 AR2103 DX2110a DO00 PY02 AO01 DX2013b PY03 AO02 DG2001 PY04
-AO03 DG2011 PY05 AO04 Dq2001 PY06 Dq2011 AO05 DX2100 PY07 AO06 DX2101 PY08 AO07
-DX2111a PY09 AO08 DX2102 PY10 AO09 DX2103 PY11 AO10 DX2112a DX2113a PY12 AO11 DG2100
-PY13 AO12 DG2110 PY14 AO13 Dq2100 PY15 Dq2110 AO14 DX2110b PY16 DX2111b AO15 DG2101
-PY17 AO16 DX2112b PY18 Dq2101 AO17 DX2113b PY19 AO18 DG2111 PY20 AO19 PY21 Dq2111
-AO20 PY22 AO21 PY23 AO22 PY24 AO23 PY25 DO24 PY26 DO25 PY27 AO26 PY28
-DO27 PY29 DO28 PY30 DO29 PY31 AO30 AO31
+Dp10 PT0 Ds11 PT1 PT2 AC1 PT3 AC0 DC2 PT4 Ds10 AC3 PT5 AC4
+Dq001 PT6 AC5 Dq000 PT7 AC6 Dp11 PM1000 AC7 Dq011 PM1010 Dp21 PM1011 Dq010
+AR1010 Ds21 AR1000 PM1001 DX1010 AR1011 PM1012 DX1000 AR1001 PM1013 Ds20 AR1012 PM1002 DX1001
+AR1013 PM1110 DX1011 AR1002 PM1003 DX1012 AR1110 PM1100 DX1013 AR1003 PM1101 DX1002 AG1010 PM1102
+DX1003 PM1111 DG1011 AG1001 PM1112 DG1000 PM1103 Dp20 PM1113 AR1100 AR1111 Dq100 AR1101 Dq101
+PM2010 AR1102 DX1100 PM2000 AR1103 DX1110 PM2001 DX1101 AR1112 PM2002 DX1102 AR2000 PM2011 DX1103
+AR2010a AR2001 PM2003 DX1111 AR1113 PM2012 DX1112 AR2002 PM2013 DG1101 AR2003 DX1113 AR2010b DG1100
+AG1111 DG1110 Dq110 AR2011a Dq111 AR2011b AR2012a PM2100 DX2010a AR2012b DX2010b AR2013a PM2110 DX2000
+AR2013b PM2101 AR2100 DX2001 PM2111 AR2110b DX2002 AR2110a PM2112 DX2003 AR2111a AR2111b PM2102 DX2011a
+AG2000 DX2012a PM2113 DX2013a DX2011b PM2103 DG2010 AR2101 Dq2000 AR2102 Dq2010 DG2001 PY00 AR2112a
+AR2112b DX2012b PY01 AO00 DX2013b Dq2001 PY02 AO01 DG2011 PY03 AR2113b DX2100 AR2113a PY04
+AO03 DO02 PY05 AR2103 DO04 PY06 AO05 Dq2011 PY07 DX2110a AO06 DX2101 PY08 AO07
+DX2102 PY09 AO08 DX2103 PY10 AO09 DX2111a PY11 DX2112a AO10 DX2113a PY12 DG2100 AO11
+PY13 DG2110 AO12 PY14 Dq2100 AO13 Dq2110 PY15 DO14 PY16 AO15 DX2110b PY17 DX2111b
+AO16 DX2112b PY18 DO17 AG2101 PY19 DO18 PY20 DX2113b AO19 PY21 DG2111 AO20 PY22
+Dq2101 AO21 Dq2111 PY23 AO22 PY24 DO23 PY25 DO24 PY26 DO25 PY27 DO26 PY28
+DO27 PY29 AO28 PY30 AO29 PY31 AO30 DO31
 """
 
 
@@ -102,13 +102,13 @@ def tile_theta_phase_rates_t2_kernel(
         def load_gain(i, g_in):
             nc.sync.dma_start(out=gains[i][:], in_=g_in.rearrange("(g p t) -> p g t", g=G, t=T))
 
-        for i, g_in in ((1, gain1), (2, gain2)):
-            nc.gpsimd.dma_start(out=gains[i][:], in_=g_in.rearrange("(g p t) -> p g t", g=G, t=T))
         load_words(1, 0, 2)
         load_blocks(0, 1)
         load_scales(1, nc.sync)
         load_blocks(1, 1)
         load_blocks(2, 2)
+        for i, g_in in ((1, gain1), (2, gain2)):
+            nc.sync.dma_start(out=gains[i][:], in_=g_in.rearrange("(g p t) -> p g t", g=G, t=T))
         load_words(1, 1, 2)
         load_blocks(4, 2)
         load_blocks(6, 2)
@@ -258,7 +258,7 @@ def tile_theta_phase_rates_t2_kernel(
             parts = 2 if width == 512 else 1
             if (s, c, h) not in grouped:
                 grouped[s, c, h] = work.tile([P, width, T], BF16, name="grouped", align_bytes=64, bufs=4)
-            run = 4 if s == 1 else 8
+            run = 4
             src = r1[c][:, h, :, :] if s == 1 else r2[c, h][:]
             m = slice(width // parts * part, width // parts * (part + 1))
             copy_out(

@@ -4,8 +4,7 @@ import concourse.mybir as mybir
 from concourse.masks import make_identity
 
 TRIALS, NEURONS, TARGETS = 1024, 1024, 2048
-SINGLE = (30, 31)
-FLOPS = 2 * TRIALS * NEURONS * (2 * NEURONS + TARGETS)
+FLOPS = 2 * TRIALS * NEURONS * (NEURONS + NEURONS + TARGETS)
 
 F32 = mybir.dt.float32
 BF16 = mybir.dt.bfloat16
@@ -14,32 +13,42 @@ I32 = mybir.dt.int32
 U8 = mybir.dt.uint8
 E4M3 = mybir.dt.float8_e4m3fn_x4
 E2M1 = mybir.dt.float4_e2m1fn_x4
-ACT = mybir.ActivationFunctionType
+RELU = mybir.ActivationFunctionType.Relu
 ALU = mybir.AluOpType
 
 P = 128
-G = 2
-T = 4
-CHUNKS = (512, 512)
-ORDER = """
-Dp10 PT0 Ds11 PT1 PT2 AC1 PT3 AC0 DC2 PT4 Ds10 AC3 PT5 AC4
-Dq001 PT6 AC5 Dq000 PT7 AC6 Dp11 PM1000 AC7 Dq011 PM1010 Dp21 PM1011 Dq010
-AR1010 Ds21 AR1000 PM1001 DX1010 AR1011 PM1012 DX1000 AR1001 PM1013 Ds20 AR1012 PM1002 DX1001
-AR1013 PM1110 DX1011 AR1002 PM1003 DX1012 AR1110 PM1100 DX1013 AR1003 PM1101 DX1002 AG1010 PM1102
-DX1003 PM1111 DG1011 AG1001 PM1112 DG1000 PM1103 Dp20 PM1113 AR1100 AR1111 Dq100 AR1101 Dq101
-PM2010 AR1102 DX1100 PM2000 AR1103 DX1110 PM2001 DX1101 AR1112 PM2002 DX1102 AR2000 PM2011 DX1103
-AR2010a AR2001 PM2003 DX1111 AR1113 PM2012 DX1112 AR2002 PM2013 DG1101 AR2003 DX1113 AR2010b DG1100
-AG1111 DG1110 Dq110 AR2011a Dq111 AR2011b AR2012a PM2100 DX2010a AR2012b DX2010b AR2013a PM2110 DX2000
-AR2013b PM2101 AR2100 DX2001 PM2111 AR2110b DX2002 AR2110a PM2112 DX2003 AR2111a AR2111b PM2102 DX2011a
-AG2000 DX2012a PM2113 DX2013a DX2011b PM2103 DG2010 AR2101 Dq2000 AR2102 Dq2010 DG2001 PY00 AR2112a
-AR2112b DX2012b PY01 AO00 DX2013b Dq2001 PY02 AO01 DG2011 PY03 AR2113b DX2100 AR2113a PY04
-AO03 DO02 PY05 AR2103 DO04 PY06 AO05 Dq2011 PY07 DX2110a AO06 DX2101 PY08 AO07
-DX2102 PY09 AO08 DX2103 PY10 AO09 DX2111a PY11 DX2112a AO10 DX2113a PY12 DG2100 AO11
-PY13 DG2110 AO12 PY14 Dq2100 AO13 Dq2110 PY15 DO14 PY16 AO15 DX2110b PY17 DX2111b
-AO16 DX2112b PY18 DO17 AG2101 PY19 DO18 PY20 DX2113b AO19 PY21 DG2111 AO20 PY22
-Dq2101 AO21 Dq2111 PY23 AO22 PY24 DO23 PY25 DO24 PY26 DO25 PY27 DO26 PY28
-DO27 PY29 AO28 PY30 AO29 PY31 AO30 DO31
-"""
+PACK = 4
+PASS = P * PACK
+GROUPS = NEURONS // PASS
+WIDE = 512
+HALVES = TRIALS // WIDE
+BLOCKS = WIDE // P
+QUARTER = WIDE // 2
+BANKS = 8
+RUN = 4
+
+ORDER = (
+    ("T0 T1 T2 T3", "C0", "p10 s10 C1 C2"),
+    ("T4 T5 T6 T7", "C3 C4 C5 C6", "s11 q000 q001 p11"),
+    ("M100 M101", "C7 R100 R100", "q010 q011 p21 X100"),
+    ("M110", "R101 R101", "X100 X101 X101"),
+    ("M111", "G1000 R110 G1010", "G1001 G1011 s21 q100"),
+    ("", "R110 R111 R111", "X110 q101 X110 p20"),
+    ("", "G1101", "s20 X111"),
+    ("M200 M201", "G1100 R200", "X111 q110"),
+    ("", "G1111 R200", "G1110 X200 q111"),
+    ("M210 M211", "R201a R201a R201b R210", "X200 X201a X201a G2000"),
+    ("", "R201b R211b R210", "G2010 q2000 q2010 X201b"),
+    ("Y0 Y1", "R211b O00 R211a R211a", "X201b G2001 O01 G2011"),
+    ("", "O10 O11", "q2001 q2011 X210"),
+    ("Y2 Y3", "O20 O21 O30", "X210 X211a X211a G2100"),
+    ("", "O31", "G2110 q2100 q2110 X211b"),
+    ("Y4 Y5", "O40 O41 O50", "G2101 q2101 X211b G2111"),
+    ("", "", "q2111 O51"),
+    ("Y6 Y7", "O60 O61", "O70"),
+    ("", "O71", ""),
+)
+NARROW_STORES = ("O71",)
 
 
 def tile_theta_phase_rates_t2_kernel(
@@ -48,286 +57,241 @@ def tile_theta_phase_rates_t2_kernel(
     nc = tc.nc
     with ExitStack() as ctx:
         keep = ctx.enter_context(tc.tile_pool(name="keep", bufs=1))
-        work = ctx.enter_context(tc.tile_pool(name="work", bufs=2))
-        psum = ctx.enter_context(tc.psum_pool(name="psum", bufs=8))
+        work = ctx.enter_context(tc.tile_pool(name="work", bufs=4))
+        psum = ctx.enter_context(tc.psum_pool(name="psum", bufs=BANKS))
         ctx.enter_context(tc.manual_schedule())
 
-        def const(name, shape, dtype):
+        def kept(name, shape, dtype):
             return keep.tile(shape, dtype, name=name, align_bytes=256)
 
-        raw_w = {}
-        raw_s = {}
-        for i in (1, 2, 3):
-            n = TARGETS if i == 3 else NEURONS
-            raw_w[i] = const(f"raw_w{i}", [P, G, 2 * n], U8)
-            raw_s[i] = const(f"raw_s{i}", [P, G, n], U8)
         words_in = {1: w1_words, 2: w2_words, 3: w3_words}
         scales_in = {1: w1_scales, 2: w2_scales, 3: w3_scales}
-        ident = const("ident", [P, P], F32)
+        columns = {1: NEURONS, 2: NEURONS, 3: TARGETS}
+        w_raw, s_raw, w_moved, s_moved = {}, {}, {}, {}
+        for s in (1, 2, 3):
+            w_raw[s] = kept(f"w_raw{s}", [P, GROUPS, 2 * columns[s]], U8)
+            s_raw[s] = kept(f"s_raw{s}", [P, GROUPS, columns[s]], U8)
+        for s in (1, 2):
+            w_moved[s] = kept(f"w_moved{s}", [P, GROUPS, GROUPS, PACK, P, 2], U8)
+            s_moved[s] = kept(f"s_moved{s}", [P, GROUPS, GROUPS, PACK, P], U8)
+        gains_in = {1: gain1, 2: gain2}
+        gains = {s: kept(f"gain{s}", [P, GROUPS, PACK], BF16) for s in (1, 2)}
+        r0, r1 = {}, {}
+        codes, planes = {}, {}
+        for h in range(HALVES):
+            r0[h] = kept(f"r0_{h}", [P, GROUPS, WIDE, PACK], BF16)
+            r1[h] = kept(f"r1_{h}", [P, GROUPS, PACK, WIDE], F32)
+            for s in (0, 1, 2):
+                codes[s, h] = kept(f"codes{s}_{h}", [P, GROUPS, WIDE], U32)
+                planes[s, h] = kept(f"planes{s}_{h}", [P, GROUPS, WIDE], U8)
+
+        ident = kept("ident", [P, P], F32)
         make_identity(nc, ident[:])
-        for i in (1, 2, 3):
-            nc.vector.memset(raw_s[i][:].rearrange("p g n -> p (g n)").bitcast(I32), 0)
+        for s in (1, 2, 3):
+            nc.vector.memset(s_raw[s][:].rearrange("p g n -> p (g n)").bitcast(I32), 0)
 
-        gains = {}
-        for i, g_in in ((1, gain1), (2, gain2)):
-            gains[i] = const(f"gain{i}", [P, G, T], BF16)
-
-        def load_scales(i, queue):
-            src = scales_in[i].bitcast(I32)
+        def load_scales(s):
             for q in range(4):
-                queue.dma_start(
-                    out=raw_s[i][32 * q : 32 * q + 4, :, :].bitcast(I32),
-                    in_=src[:, 4 * q : 4 * q + 4, :].rearrange("g q n -> q g n"),
+                nc.sync.dma_start(
+                    out=s_raw[s][32 * q : 32 * q + 4, :, :].bitcast(I32),
+                    in_=scales_in[s].bitcast(I32)[:, 4 * q : 4 * q + 4, :].rearrange("g q n -> q g n"),
                 )
 
-        def load_words(i, part, parts):
-            size_w = words_in[i].shape[2] // 4 // parts
-            cols = slice(size_w * part, size_w * (part + 1))
+        def load_words(s, part, parts):
+            per_group = 2 * columns[s] // 4 // parts
+            piece = slice(per_group * part, per_group * (part + 1))
+            tile = w_raw[s][:].rearrange("p g n -> p (g n)").bitcast(I32).rearrange("p (g n) -> p g n", g=GROUPS)
             nc.sync.dma_start(
-                out=raw_w[i][:].rearrange("p g n -> p (g n)").bitcast(I32).rearrange("p (g n) -> p g n", g=G)[:, :, cols],
-                in_=words_in[i].bitcast(I32)[:, :, cols].rearrange("g p n -> p g n"),
+                out=tile[:, :, piece], in_=words_in[s].bitcast(I32)[:, :, piece].rearrange("g p n -> p g n")
             )
 
-        n_blocks = TRIALS // P
         x = {}
 
-        def load_blocks(b, count):
-            tile = const(f"x{b}", [P, count, NEURONS], BF16)
+        def load_rates(first, count):
+            tile = kept(f"x{first}", [P, count, NEURONS], BF16)
             for i in range(count):
-                x[b + i] = tile[:, i, :]
-            nc.sync.dma_start(
-                out=tile[:], in_=rates[b * P : (b + count) * P, :].rearrange("(i p) n -> p i n", p=P)
-            )
-
-        def load_gain(i, g_in):
-            nc.sync.dma_start(out=gains[i][:], in_=g_in.rearrange("(g p t) -> p g t", g=G, t=T))
+                x[first + i] = tile[:, i, :]
+            rows = rates[first * P : (first + count) * P, :]
+            nc.sync.dma_start(out=tile[:], in_=rows.rearrange("(i p) n -> p i n", p=P))
 
         load_words(1, 0, 2)
-        load_blocks(0, 1)
-        load_scales(1, nc.sync)
-        load_blocks(1, 1)
-        load_blocks(2, 2)
-        for i, g_in in ((1, gain1), (2, gain2)):
-            nc.sync.dma_start(out=gains[i][:], in_=g_in.rearrange("(g p t) -> p g t", g=G, t=T))
+        load_rates(0, 1)
+        load_scales(1)
+        load_rates(1, 1)
+        load_rates(2, 2)
+        for s in (1, 2):
+            nc.sync.dma_start(out=gains[s][:], in_=gains_in[s].rearrange("(g p t) -> p g t", g=GROUPS, t=PACK))
         load_words(1, 1, 2)
-        load_blocks(4, 2)
-        load_blocks(6, 2)
-        load_scales(2, nc.sync)
+        load_rates(4, 2)
+        load_rates(6, 2)
+        load_scales(2)
         load_words(2, 0, 1)
-        load_scales(3, nc.sync)
+        load_scales(3)
         load_words(3, 0, 1)
 
-        size = {}
-        sign = {}
-
-        def prepare_gain(i):
-            flat = gains[i][:].rearrange("p g t -> p (g t)")
-            size[i] = const(f"size{i}", [P, G * T], F32)
-            sign[i] = const(f"sign{i}", [P, G * T], F32)
-            nc.scalar.activation(out=size[i][:], in_=flat, func=ACT.Abs)
-            nc.vector.tensor_scalar(
-                out=sign[i][:], in0=flat, scalar1=0.0, scalar2=2.0, op0=ALU.is_ge, op1=ALU.mult
-            )
-            nc.vector.tensor_scalar_add(sign[i][:], sign[i][:], -1.0)
-
-        per_w = {}
-        per_s = {}
-        for i in (1, 2):
-            per_w[i] = const(f"per_w{i}", [P, G, G, T, P, 2], U8)
-            per_s[i] = const(f"per_s{i}", [P, G, G, T, P], U8)
-
-        def permute_words(i, h):
-            for g in range(G):
-                nc.vector.tensor_copy(
-                    out=per_w[i][:, g, h, :, :, :],
-                    in_=raw_w[i][:, g, 1024 * h : 1024 * h + 1024].rearrange("p (j t b) -> p t j b", t=T, b=2),
-                )
-
-        def permute_scales(i, h):
-            nc.vector.tensor_copy(
-                out=per_s[i][:, :, h, :, :],
-                in_=raw_s[i][:, :, 512 * h : 512 * h + 512].rearrange("p g (j t) -> p g t j", t=T),
-            )
-
-        starts = [sum(CHUNKS[:c]) for c in range(len(CHUNKS))]
-        rt = {}
-        codes = {}
-        planes = {}
-        r1 = {}
-        for c, width in enumerate(CHUNKS):
-            rt[c] = const(f"rt{c}", [P, G, width, T], BF16)
-            r1[c] = const(f"r1_{c}", [P, G, T, width], F32)
-            for s in (0, 1, 2):
-                codes[s, c] = const(f"codes{s}_{c}", [P, G, width], U32)
-                planes[s, c] = const(f"planes{s}_{c}", [P, G, width], U8)
+        banks = {}
+        v = {}
+        r2 = {}
+        grouped = {}
+        y = {}
 
         def bank():
-            return psum.tile([P, 512], F32, name="bank")
+            return psum.tile([P, WIDE], F32, name="bank")
 
-        def copy_out(use_v, dst, src):
-            if use_v:
+        def copy(engine, dst, src):
+            if engine == "vector":
                 nc.vector.tensor_copy(out=dst, in_=src)
             else:
                 nc.scalar.copy(out=dst, in_=src)
 
-        def words_out(c):
-            return rt[c][:].rearrange("p g m t -> p (g m t)").bitcast(F32).rearrange("p (g m u) -> p g m u", g=G, u=2)
+        def trials(part):
+            return slice(0, WIDE) if part is None else slice(QUARTER * part, QUARTER * (part + 1))
 
-        banks = {}
+        def move_words(s, g):
+            for k in range(GROUPS):
+                cols = w_raw[s][:, k, 2 * PASS * g : 2 * PASS * (g + 1)]
+                nc.vector.tensor_copy(
+                    out=w_moved[s][:, k, g, :, :, :], in_=cols.rearrange("q (p t b) -> q t p b", t=PACK, b=2)
+                )
 
-        def transpose(blk):
-            words = x[blk].bitcast(F32)
-            acc = banks[blk] = bank()
-            for g in range(G):
+        def move_scales(s, g):
+            cols = s_raw[s][:, :, PASS * g : PASS * (g + 1)]
+            nc.vector.tensor_copy(out=s_moved[s][:, :, g, :, :], in_=cols.rearrange("q k (p t) -> q k t p", t=PACK))
+
+        def transpose(b):
+            words = x[b].bitcast(F32)
+            banks["T", b] = bank()
+            for g in range(GROUPS):
                 for u in range(2):
-                    k = 2 * g + u
+                    i = 2 * g + u
                     nc.tensor.transpose(
-                        acc[:, k * P : (k + 1) * P], words[:, 256 * g + u : 256 * (g + 1) : 2], ident[:]
+                        banks["T", b][:, i * P : (i + 1) * P],
+                        words[:, PASS // 2 * g + u : PASS // 2 * (g + 1) : 2],
+                        ident[:],
                     )
 
-        def chunk_of(blk):
-            c = max(c for c in range(len(CHUNKS)) if starts[c] <= blk * P)
-            return c, blk - starts[c] // P
-
-        def copy_turned(use_v, blk):
-            c, b = chunk_of(blk)
-            copy_out(
-                use_v,
-                words_out(c)[:, :, b * P : (b + 1) * P, :],
-                banks.pop(blk)[:].rearrange("p (g u m) -> p g m u", g=G, u=2),
+        def copy_turned(engine, b):
+            h, i = divmod(b, BLOCKS)
+            words = r0[h][:].rearrange("p g m t -> p (g m t)").bitcast(F32).rearrange(
+                "p (g m u) -> p g m u", g=GROUPS, u=2
             )
+            turned = banks.pop(("T", b))[:].rearrange("p (g u m) -> p g m u", g=GROUPS, u=2)
+            copy(engine, words[:, :, i * P : (i + 1) * P, :], turned)
 
-        def quantise(s, c, g, half=None):
-            m = half_of(CHUNKS[c], half)
-            src = rt[c][:, g, m, :] if s == 0 else grouped[s, c, g][:, m, :]
+        def quantise(s, h, g, part):
+            m = trials(part)
+            values = r0[h][:, g, m, :] if s == 0 else grouped[s, h, g][:, m, :]
             nc.vector.quantize_mx(
-                out=codes[s, c][:, g, m].bitcast(E4M3), scales=planes[s, c][:, g, m], in_=src.rearrange("p m t -> p (m t)")
+                out=codes[s, h][:, g, m].bitcast(E4M3),
+                scales=planes[s, h][:, g, m],
+                in_=values.rearrange("p m t -> p (m t)"),
             )
 
-        v = {}
-        r2 = {}
-        grouped = {}
-
-        def multiply(s, c, h, t):
-            width = CHUNKS[c]
-            step = 512 if width == 512 else 128
-            acc = banks[s, c, h, t] = bank()
-            for n0 in range(0, width, step):
-                for g in range(G):
+        def multiply(s, h, g):
+            for t in range(PACK):
+                banks[s, h, g, t] = bank()
+                for k in range(GROUPS):
                     nc.tensor.matmul_mx(
-                        out=acc[:, n0 : n0 + step],
-                        lhsT=per_w[s][:, g, h, t, :, :].rearrange("p j b -> p (j b)").bitcast(E2M1),
-                        lhsT_scale=per_s[s][:, g, h, t, :],
-                        rhs=codes[s - 1, c][:, g, n0 : n0 + step].bitcast(E4M3),
-                        rhs_scale=planes[s - 1, c][:, g, n0 : n0 + step],
-                        start=(g == 0),
-                        stop=(g == G - 1),
+                        out=banks[s, h, g, t][:],
+                        lhsT=w_moved[s][:, k, g, t, :, :].rearrange("q p b -> q (p b)").bitcast(E2M1),
+                        lhsT_scale=s_moved[s][:, k, g, t, :],
+                        rhs=codes[s - 1, h][:, k, :].bitcast(E4M3),
+                        rhs_scale=planes[s - 1, h][:, k, :],
+                        start=(k == 0),
+                        stop=(k == GROUPS - 1),
                     )
 
-        def half_of(width, half):
-            return slice(0, width) if half is None else slice(width // 2 * half, width // 2 * (half + 1))
+        def relu(s, h, g, t, part):
+            m = trials(part)
+            v[s, h, g, t, part] = work.tile([P, WIDE], F32, name="v", bufs=15)
+            nc.scalar.activation(out=v[s, h, g, t, part][:, m], in_=banks[s, h, g, t][:, m], func=RELU)
 
-        def relu(s, c, h, t, half):
-            width = CHUNKS[c]
-            m = half_of(width, half)
-            v[s, c, h, t, half] = work.tile([P, width], F32, name="v", bufs=15)
-            j = h * T + t
-            nc.scalar.activation(
-                out=v[s, c, h, t, half][:, m],
-                in_=banks[s, c, h, t][:, m],
-                func=ACT.Relu,
-                scale=size[s][:, j : j + 1],
-            )
-
-        def add(s, c, h, t, half):
-            m = half_of(CHUNKS[c], half)
-            if s == 2 and (c, h) not in r2:
-                r2[c, h] = work.tile([P, T, CHUNKS[c]], BF16, name="r2", bufs=4)
-            j = h * T + t
+        def add(s, h, g, t, part):
+            m = trials(part)
+            if s == 2 and (h, g) not in r2:
+                r2[h, g] = work.tile([P, PACK, WIDE], BF16, name="r2")
             nc.vector.scalar_tensor_tensor(
-                out=r1[c][:, h, t, m] if s == 1 else r2[c, h][:, t, m],
-                in0=v[s, c, h, t, half][:, m],
-                scalar=sign[s][:, j : j + 1],
-                in1=rt[c][:, h, m, t] if s == 1 else r1[c][:, h, t, m],
+                out=r1[h][:, g, t, m] if s == 1 else r2[h, g][:, t, m],
+                in0=v[s, h, g, t, part][:, m],
+                scalar=gains[s][:, g, t : t + 1],
+                in1=r0[h][:, g, m, t] if s == 1 else r1[h][:, g, t, m],
                 op0=ALU.mult,
                 op1=ALU.add,
             )
 
-        def cast(use_v, s, c, h, part):
-            width = CHUNKS[c]
-            parts = 2 if width == 512 else 1
-            if (s, c, h) not in grouped:
-                grouped[s, c, h] = work.tile([P, width, T], BF16, name="grouped", align_bytes=64, bufs=4)
-            run = 4
-            src = r1[c][:, h, :, :] if s == 1 else r2[c, h][:]
-            m = slice(width // parts * part, width // parts * (part + 1))
-            copy_out(
-                use_v,
-                grouped[s, c, h][:, m, :].rearrange("p (c i) t -> p c t i", i=run),
-                src[:, :, m].rearrange("p t (c i) -> p c t i", i=run),
+        def interleave(engine, s, h, g, part):
+            if (s, h, g) not in grouped:
+                grouped[s, h, g] = work.tile([P, WIDE, PACK], BF16, name="grouped", align_bytes=64)
+            m = trials(part)
+            source = r1[h][:, g, :, :] if s == 1 else r2[h, g][:]
+            copy(
+                engine,
+                grouped[s, h, g][:, m, :].rearrange("p (c i) t -> p c t i", i=RUN),
+                source[:, :, m].rearrange("p t (c i) -> p c t i", i=RUN),
             )
 
-        ys = {}
+        def multiply_targets(b):
+            h, i = divmod(b, BLOCKS)
+            m = slice(i * P, (i + 1) * P)
+            for n in range(TARGETS // WIDE):
+                banks["Y", b, n] = bank()
+                for k in range(GROUPS):
+                    nc.tensor.matmul_mx(
+                        out=banks["Y", b, n][:],
+                        lhsT=codes[2, h][:, k, m].bitcast(E4M3),
+                        lhsT_scale=planes[2, h][:, k, m],
+                        rhs=w_raw[3][:, k, 2 * WIDE * n : 2 * WIDE * (n + 1)].bitcast(E2M1),
+                        rhs_scale=s_raw[3][:, k, WIDE * n : WIDE * (n + 1)],
+                        start=(k == 0),
+                        stop=(k == GROUPS - 1),
+                    )
 
-        def y_mul(i):
-            b, n = divmod(i, 4)
-            c, m0 = chunk_of(b)
-            m = slice(m0 * P, (m0 + 1) * P)
-            acc = banks["y", i] = bank()
-            for g in range(G):
-                nc.tensor.matmul_mx(
-                    out=acc[:],
-                    lhsT=codes[2, c][:, g, m].bitcast(E4M3),
-                    lhsT_scale=planes[2, c][:, g, m],
-                    rhs=raw_w[3][:, g, 1024 * n : 1024 * n + 1024].bitcast(E2M1),
-                    rhs_scale=raw_s[3][:, g, 512 * n : 512 * n + 512],
-                    start=(g == 0),
-                    stop=(g == G - 1),
-                )
+        def store(engine, b, j, narrow):
+            pair = work.tile([P, 2 * WIDE], F32, name="y", bufs=7)
+            rows = slice(b * P, (b + 1) * P)
+            for i in range(2):
+                n = 2 * j + i
+                piece = slice(WIDE * i, WIDE * (i + 1))
+                copy(engine, pair[:, piece], banks.pop(("Y", b, n))[:])
+                if narrow:
+                    nc.sync.dma_start(out=out[rows, WIDE * n : WIDE * (n + 1)], in_=pair[:, piece])
+            if not narrow:
+                nc.sync.dma_start(out=out[rows, 2 * WIDE * j : 2 * WIDE * (j + 1)], in_=pair[:])
 
-        def y_out(use_v, i):
-            b, n = divmod(i, 4)
-            pair = i // 2
-            if pair not in ys:
-                ys[pair] = [work.tile([P, 1024], F32, name="y", bufs=7), 0]
-            ys[pair][1] += 1
-            half = slice(512 * (n % 2), 512 * (n % 2) + 512)
-            copy_out(use_v, ys[pair][0][:, half], banks.pop(("y", i))[:])
-            if i in SINGLE:
-                nc.sync.dma_start(out=out[b * P : (b + 1) * P, 512 * n : 512 * n + 512], in_=ys[pair][0][:, half])
-            elif ys[pair][1] == 2:
-                both = slice(1024 * (n // 2), 1024 * (n // 2) + 1024)
-                nc.sync.dma_start(out=out[b * P : (b + 1) * P, both], in_=ys[pair][0][:])
+        issued = {}
 
-        ready = False
-        for token in ORDER.split():
-            use_v = token[0] == "D"
-            kind = token[1]
-            half = {"a": 0, "b": 1}.get(token[-1])
-            a = [int(ch) for ch in token[2:] if ch not in "ab"]
-            if kind == "R" and not ready:
-                prepare_gain(1)
-                prepare_gain(2)
-                ready = True
-            if kind == "p":
-                permute_words(*a)
-            elif kind == "s":
-                permute_scales(*a)
-            elif kind == "T":
-                transpose(*a)
-            elif kind == "C":
-                copy_turned(use_v, *a)
-            elif kind == "q":
-                quantise(*a)
-            elif kind == "M":
-                multiply(*a)
-            elif kind == "R":
-                relu(*a, half)
-            elif kind == "X":
-                add(*a, half)
-            elif kind == "G":
-                cast(use_v, *a)
-            elif kind == "Y":
-                y_mul(a[0] * 10 + a[1])
-            elif kind == "O":
-                y_out(use_v, a[0] * 10 + a[1])
+        def next_two(token):
+            first = issued.get(token, 0)
+            issued[token] = first + 2
+            return range(first, first + 2)
+
+        for row in ORDER:
+            for engine, tokens in zip(("tensor", "scalar", "vector"), row):
+                for token in tokens.split():
+                    kind = token[0]
+                    part = {"a": 0, "b": 1}.get(token[-1])
+                    a = [int(digit) for digit in token[1:] if digit not in "ab"]
+                    if kind == "p":
+                        move_words(*a)
+                    elif kind == "s":
+                        move_scales(*a)
+                    elif kind == "T":
+                        transpose(*a)
+                    elif kind == "C":
+                        copy_turned(engine, *a)
+                    elif kind == "q":
+                        quantise(a[0], a[1], a[2], a[3] if len(a) == 4 else None)
+                    elif kind == "M":
+                        multiply(*a)
+                    elif kind == "R":
+                        for t in next_two(token):
+                            relu(a[0], a[1], a[2], t, part)
+                    elif kind == "X":
+                        for t in next_two(token):
+                            add(a[0], a[1], a[2], t, part)
+                    elif kind == "G":
+                        interleave(engine, *a)
+                    elif kind == "Y":
+                        multiply_targets(*a)
+                    else:
+                        store(engine, a[0], a[1], token in NARROW_STORES)

from contextlib import ExitStack

import concourse.mybir as mybir
from concourse.masks import make_identity

TRIALS, NEURONS, TARGETS = 1024, 1024, 2048
FLOPS = 2 * TRIALS * NEURONS * (NEURONS + NEURONS + TARGETS)

F32 = mybir.dt.float32
BF16 = mybir.dt.bfloat16
U32 = mybir.dt.uint32
I32 = mybir.dt.int32
U8 = mybir.dt.uint8
E4M3 = mybir.dt.float8_e4m3fn_x4
E2M1 = mybir.dt.float4_e2m1fn_x4
RELU = mybir.ActivationFunctionType.Relu
ALU = mybir.AluOpType

P = 128
PACK = 4
PASS = P * PACK
GROUPS = NEURONS // PASS
WIDE = 512
HALVES = TRIALS // WIDE
BLOCKS = WIDE // P
QUARTER = WIDE // 2
BANKS = 8
RUN = 4

ORDER = (
    ("T0 T1 T2 T3", "C0", "p10 s10 C1 C2"),
    ("T4 T5 T6 T7", "C3 C4 C5 C6", "s11 q000 q001 p11"),
    ("M100 M101", "C7 R100 R100", "q010 q011 p21 X100"),
    ("M110", "R101 R101", "X100 X101 X101"),
    ("M111", "G1000 R110 G1010", "G1001 G1011 s21 q100"),
    ("", "R110 R111 R111", "X110 q101 X110 p20"),
    ("", "G1101", "s20 X111"),
    ("M200 M201", "G1100 R200", "X111 q110"),
    ("", "G1111 R200", "G1110 X200 q111"),
    ("M210 M211", "R201a R201a R201b R210", "X200 X201a X201a G2000"),
    ("", "R201b R211b R210", "G2010 q2000 q2010 X201b"),
    ("Y0 Y1", "R211b O00 R211a R211a", "X201b G2001 O01 G2011"),
    ("", "O10 O11", "q2001 q2011 X210"),
    ("Y2 Y3", "O20 O21 O30", "X210 X211a X211a G2100"),
    ("", "O31", "G2110 q2100 q2110 X211b"),
    ("Y4 Y5", "O40 O41 O50", "G2101 q2101 X211b G2111"),
    ("", "", "q2111 O51"),
    ("Y6 Y7", "O60 O61", "O70"),
    ("", "O71", ""),
)
NARROW_STORES = ("O71",)


def tile_theta_phase_rates_t2_kernel(
    tc, rates, gain1, gain2, w1_words, w1_scales, w2_words, w2_scales, w3_words, w3_scales, out
):
    nc = tc.nc
    with ExitStack() as ctx:
        keep = ctx.enter_context(tc.tile_pool(name="keep", bufs=1))
        work = ctx.enter_context(tc.tile_pool(name="work", bufs=4))
        psum = ctx.enter_context(tc.psum_pool(name="psum", bufs=BANKS))
        ctx.enter_context(tc.manual_schedule())

        def kept(name, shape, dtype):
            return keep.tile(shape, dtype, name=name, align_bytes=256)

        words_in = {1: w1_words, 2: w2_words, 3: w3_words}
        scales_in = {1: w1_scales, 2: w2_scales, 3: w3_scales}
        columns = {1: NEURONS, 2: NEURONS, 3: TARGETS}
        w_raw, s_raw, w_moved, s_moved = {}, {}, {}, {}
        for s in (1, 2, 3):
            w_raw[s] = kept(f"w_raw{s}", [P, GROUPS, 2 * columns[s]], U8)
            s_raw[s] = kept(f"s_raw{s}", [P, GROUPS, columns[s]], U8)
        for s in (1, 2):
            w_moved[s] = kept(f"w_moved{s}", [P, GROUPS, GROUPS, PACK, P, 2], U8)
            s_moved[s] = kept(f"s_moved{s}", [P, GROUPS, GROUPS, PACK, P], U8)
        gains_in = {1: gain1, 2: gain2}
        gains = {s: kept(f"gain{s}", [P, GROUPS, PACK], BF16) for s in (1, 2)}
        r0, r1 = {}, {}
        codes, planes = {}, {}
        for h in range(HALVES):
            r0[h] = kept(f"r0_{h}", [P, GROUPS, WIDE, PACK], BF16)
            r1[h] = kept(f"r1_{h}", [P, GROUPS, PACK, WIDE], F32)
            for s in (0, 1, 2):
                codes[s, h] = kept(f"codes{s}_{h}", [P, GROUPS, WIDE], U32)
                planes[s, h] = kept(f"planes{s}_{h}", [P, GROUPS, WIDE], U8)

        ident = kept("ident", [P, P], F32)
        make_identity(nc, ident[:])
        for s in (1, 2, 3):
            nc.vector.memset(s_raw[s][:].rearrange("p g n -> p (g n)").bitcast(I32), 0)

        def load_scales(s):
            for q in range(4):
                nc.sync.dma_start(
                    out=s_raw[s][32 * q : 32 * q + 4, :, :].bitcast(I32),
                    in_=scales_in[s].bitcast(I32)[:, 4 * q : 4 * q + 4, :].rearrange("g q n -> q g n"),
                )

        def load_words(s, part, parts):
            per_group = 2 * columns[s] // 4 // parts
            piece = slice(per_group * part, per_group * (part + 1))
            tile = w_raw[s][:].rearrange("p g n -> p (g n)").bitcast(I32).rearrange("p (g n) -> p g n", g=GROUPS)
            nc.sync.dma_start(
                out=tile[:, :, piece], in_=words_in[s].bitcast(I32)[:, :, piece].rearrange("g p n -> p g n")
            )

        x = {}

        def load_rates(first, count):
            tile = kept(f"x{first}", [P, count, NEURONS], BF16)
            for i in range(count):
                x[first + i] = tile[:, i, :]
            rows = rates[first * P : (first + count) * P, :]
            nc.sync.dma_start(out=tile[:], in_=rows.rearrange("(i p) n -> p i n", p=P))

        load_words(1, 0, 2)
        load_rates(0, 1)
        load_scales(1)
        load_rates(1, 1)
        load_rates(2, 2)
        for s in (1, 2):
            nc.sync.dma_start(out=gains[s][:], in_=gains_in[s].rearrange("(g p t) -> p g t", g=GROUPS, t=PACK))
        load_words(1, 1, 2)
        load_rates(4, 2)
        load_rates(6, 2)
        load_scales(2)
        load_words(2, 0, 1)
        load_scales(3)
        load_words(3, 0, 1)

        banks = {}
        v = {}
        r2 = {}
        grouped = {}
        y = {}

        def bank():
            return psum.tile([P, WIDE], F32, name="bank")

        def copy(engine, dst, src):
            if engine == "vector":
                nc.vector.tensor_copy(out=dst, in_=src)
            else:
                nc.scalar.copy(out=dst, in_=src)

        def trials(part):
            return slice(0, WIDE) if part is None else slice(QUARTER * part, QUARTER * (part + 1))

        def move_words(s, g):
            for k in range(GROUPS):
                cols = w_raw[s][:, k, 2 * PASS * g : 2 * PASS * (g + 1)]
                nc.vector.tensor_copy(
                    out=w_moved[s][:, k, g, :, :, :], in_=cols.rearrange("q (p t b) -> q t p b", t=PACK, b=2)
                )

        def move_scales(s, g):
            cols = s_raw[s][:, :, PASS * g : PASS * (g + 1)]
            nc.vector.tensor_copy(out=s_moved[s][:, :, g, :, :], in_=cols.rearrange("q k (p t) -> q k t p", t=PACK))

        def transpose(b):
            words = x[b].bitcast(F32)
            banks["T", b] = bank()
            for g in range(GROUPS):
                for u in range(2):
                    i = 2 * g + u
                    nc.tensor.transpose(
                        banks["T", b][:, i * P : (i + 1) * P],
                        words[:, PASS // 2 * g + u : PASS // 2 * (g + 1) : 2],
                        ident[:],
                    )

        def copy_turned(engine, b):
            h, i = divmod(b, BLOCKS)
            words = r0[h][:].rearrange("p g m t -> p (g m t)").bitcast(F32).rearrange(
                "p (g m u) -> p g m u", g=GROUPS, u=2
            )
            turned = banks.pop(("T", b))[:].rearrange("p (g u m) -> p g m u", g=GROUPS, u=2)
            copy(engine, words[:, :, i * P : (i + 1) * P, :], turned)

        def quantise(s, h, g, part):
            m = trials(part)
            values = r0[h][:, g, m, :] if s == 0 else grouped[s, h, g][:, m, :]
            nc.vector.quantize_mx(
                out=codes[s, h][:, g, m].bitcast(E4M3),
                scales=planes[s, h][:, g, m],
                in_=values.rearrange("p m t -> p (m t)"),
            )

        def multiply(s, h, g):
            for t in range(PACK):
                banks[s, h, g, t] = bank()
                for k in range(GROUPS):
                    nc.tensor.matmul_mx(
                        out=banks[s, h, g, t][:],
                        lhsT=w_moved[s][:, k, g, t, :, :].rearrange("q p b -> q (p b)").bitcast(E2M1),
                        lhsT_scale=s_moved[s][:, k, g, t, :],
                        rhs=codes[s - 1, h][:, k, :].bitcast(E4M3),
                        rhs_scale=planes[s - 1, h][:, k, :],
                        start=(k == 0),
                        stop=(k == GROUPS - 1),
                    )

        def relu(s, h, g, t, part):
            m = trials(part)
            v[s, h, g, t, part] = work.tile([P, WIDE], F32, name="v", bufs=15)
            nc.scalar.activation(out=v[s, h, g, t, part][:, m], in_=banks[s, h, g, t][:, m], func=RELU)

        def add(s, h, g, t, part):
            m = trials(part)
            if s == 2 and (h, g) not in r2:
                r2[h, g] = work.tile([P, PACK, WIDE], BF16, name="r2")
            nc.vector.scalar_tensor_tensor(
                out=r1[h][:, g, t, m] if s == 1 else r2[h, g][:, t, m],
                in0=v[s, h, g, t, part][:, m],
                scalar=gains[s][:, g, t : t + 1],
                in1=r0[h][:, g, m, t] if s == 1 else r1[h][:, g, t, m],
                op0=ALU.mult,
                op1=ALU.add,
            )

        def interleave(engine, s, h, g, part):
            if (s, h, g) not in grouped:
                grouped[s, h, g] = work.tile([P, WIDE, PACK], BF16, name="grouped", align_bytes=64)
            m = trials(part)
            source = r1[h][:, g, :, :] if s == 1 else r2[h, g][:]
            copy(
                engine,
                grouped[s, h, g][:, m, :].rearrange("p (c i) t -> p c t i", i=RUN),
                source[:, :, m].rearrange("p t (c i) -> p c t i", i=RUN),
            )

        def multiply_targets(b):
            h, i = divmod(b, BLOCKS)
            m = slice(i * P, (i + 1) * P)
            for n in range(TARGETS // WIDE):
                banks["Y", b, n] = bank()
                for k in range(GROUPS):
                    nc.tensor.matmul_mx(
                        out=banks["Y", b, n][:],
                        lhsT=codes[2, h][:, k, m].bitcast(E4M3),
                        lhsT_scale=planes[2, h][:, k, m],
                        rhs=w_raw[3][:, k, 2 * WIDE * n : 2 * WIDE * (n + 1)].bitcast(E2M1),
                        rhs_scale=s_raw[3][:, k, WIDE * n : WIDE * (n + 1)],
                        start=(k == 0),
                        stop=(k == GROUPS - 1),
                    )

        def store(engine, b, j, narrow):
            pair = work.tile([P, 2 * WIDE], F32, name="y", bufs=7)
            rows = slice(b * P, (b + 1) * P)
            for i in range(2):
                n = 2 * j + i
                piece = slice(WIDE * i, WIDE * (i + 1))
                copy(engine, pair[:, piece], banks.pop(("Y", b, n))[:])
                if narrow:
                    nc.sync.dma_start(out=out[rows, WIDE * n : WIDE * (n + 1)], in_=pair[:, piece])
            if not narrow:
                nc.sync.dma_start(out=out[rows, 2 * WIDE * j : 2 * WIDE * (j + 1)], in_=pair[:])

        issued = {}

        def next_two(token):
            first = issued.get(token, 0)
            issued[token] = first + 2
            return range(first, first + 2)

        for row in ORDER:
            for engine, tokens in zip(("tensor", "scalar", "vector"), row):
                for token in tokens.split():
                    kind = token[0]
                    part = {"a": 0, "b": 1}.get(token[-1])
                    a = [int(digit) for digit in token[1:] if digit not in "ab"]
                    if kind == "p":
                        move_words(*a)
                    elif kind == "s":
                        move_scales(*a)
                    elif kind == "T":
                        transpose(*a)
                    elif kind == "C":
                        copy_turned(engine, *a)
                    elif kind == "q":
                        quantise(a[0], a[1], a[2], a[3] if len(a) == 4 else None)
                    elif kind == "M":
                        multiply(*a)
                    elif kind == "R":
                        for t in next_two(token):
                            relu(a[0], a[1], a[2], t, part)
                    elif kind == "X":
                        for t in next_two(token):
                            add(a[0], a[1], a[2], t, part)
                    elif kind == "G":
                        interleave(engine, *a)
                    elif kind == "Y":
                        multiply_targets(*a)
                    else:
                        store(engine, a[0], a[1], token in NARROW_STORES)
